import numpy as np, ml_dtypes
CORES = [34,162,290,418,42,426]
N = 6
KT, C = 1, 128
B = 1
def setup_inputs(rng):
    return {"x": rng.standard_normal((N, 128, KT * C), dtype=np.float32).astype(ml_dtypes.bfloat16)}
def setup_inputs_big(rng):
    d = setup_inputs(rng)
    for k in ("x",): d[k] = (d[k].astype(np.float32) * 1024.0).astype(d[k].dtype)
    return d
def setup_inputs_small(rng):
    d = setup_inputs(rng)
    for k in ("x",): d[k] = (d[k].astype(np.float32) * (1 / 1024.0)).astype(d[k].dtype)
    return d
def setup_inputs_apart(rng):
    d = setup_inputs(rng)
    f = (10.0 ** rng.permutation(np.linspace(-1.5, 1.5, N))).astype(np.float32).reshape(N, 1, 1)
    for k in ("x",): d[k] = (d[k].astype(np.float32) * f).astype(d[k].dtype)
    return d
def reference(x):
    X = x.astype(np.float64)
    y = np.full((N, C, (2 * B + 1) * C), np.nan)
    for r in range(N):
        for i in range(2 * B + 1):
            s = (r + i - B) % N
            if s != r: y[r][:, C * i:C * i + C] = sum(X[r][:, C * t:C * t + C].T @ X[s][:, C * t:C * t + C] for t in range(KT))
    return {"y": y.astype(ml_dtypes.bfloat16 if x.dtype != np.float64 else np.float64)}

@@ -1,0 +1,62 @@
+from concourse.bass import DstId, RemoteDMATransfer
+
+C = 128
+ENGINES_A_TRANSFER = 4
+
+SCRATCH = {
+    "xs": ("sbuf", [128, C], "bfloat16"),
+    "land_p": ("sbuf", [128, C], "bfloat16"),
+    "land_n": ("sbuf", [128, C], "bfloat16"),
+    "out_p": ("sbuf", [128, C], "bfloat16"),
+    "out_n": ("sbuf", [128, C], "bfloat16"),
+    "ps_p": ("psum", [128, 512], "float32"),
+    "ps_n": ("psum", [128, 512], "float32"),
+}
+SEMAPHORES = ["loaded", "sent", "from_p", "from_n", "mm_p", "mm_n", "cp_p", "cp_n", "st_p", "st_n"]
+
+
+def _engines(mask, first, count):
+    bits = [b for b in range(mask.bit_length()) if (mask >> b) & 1][first:first + count]
+    return sum(1 << b for b in bits)
+
+
+def _links(topo, a, b):
+    return int(topo.rack(topo.host(a)) != topo.rack(topo.host(b))) + int(topo.chip(a) != topo.chip(b))
+
+
+def rank_program(g, core, T, topo):
+    rank = T.rank_of(core)
+    if rank is None:
+        return
+    n = len(T.cores)
+    prev, nxt = T.cores[(rank - 1) % n], T.cores[(rank + 1) % n]
+    k = ENGINES_A_TRANSFER
+    S = T.sem
+
+    g.sync.dma_start(T.xs[:], T.x[:]).then_inc(S.loaded, 16)
+
+    g.wait_ge(S.loaded, 16)
+    transfers = []
+    for i, (dst, land, sem) in enumerate(((nxt, T.land_p, S.from_p), (prev, T.land_n, S.from_n))):
+        rid, pid = topo.addr(dst, core)
+        transfers.append(RemoteDMATransfer(dst_ids=[DstId(rid=rid, pnc=pid)],
+                                           dma_engine_mask=_engines(topo.mask(core, dst), i * k, k),
+                                           remote_sem=sem, src=T.xs[:], dst=land[:]))
+    g.remote_dma_fused(transfers, local_sem=S.sent)
+
+    blocks = [
+        (prev, T.land_p, S.from_p, T.ps_p, S.mm_p, T.out_p, S.cp_p, S.st_p, 0),
+        (nxt, T.land_n, S.from_n, T.ps_n, S.mm_n, T.out_n, S.cp_n, S.st_n, 2),
+    ]
+    blocks.sort(key=lambda b: _links(topo, b[0], core))
+    g.tensor.wait_ge(S.loaded, 16)
+    for q, (src, land, arrived, ps, mm, out, cp, st, blk) in zip((g.sync, g.scalar), blocks):
+        g.tensor.wait_ge(arrived, k)
+        g.tensor.matmul(ps[:, 0:C], T.xs[:], land[:], True, True).then_inc(mm, 1)
+        g.vector.wait_ge(mm, 1)
+        g.vector.tensor_copy(out[:], ps[:, 0:C]).then_inc(cp, 1)
+        q.wait_ge(cp, 1)
+        q.dma_start(T.y[:, blk * C:(blk + 1) * C], out[:]).then_inc(st, 16)
+        q.wait_ge(st, 16)
+
+    g.wait_ge(S.sent, 2 * k)

@@ -1,62 +1,91 @@
-from concourse.bass import DstId, RemoteDMATransfer
-
 C = 128
-ENGINES_A_TRANSFER = 4
+H = C // 2
 
 SCRATCH = {
+    "xd": ("dram", [128, C], "bfloat16"),
     "xs": ("sbuf", [128, C], "bfloat16"),
-    "land_p": ("sbuf", [128, C], "bfloat16"),
-    "land_n": ("sbuf", [128, C], "bfloat16"),
-    "out_p": ("sbuf", [128, C], "bfloat16"),
-    "out_n": ("sbuf", [128, C], "bfloat16"),
-    "ps_p": ("psum", [128, 512], "float32"),
-    "ps_n": ("psum", [128, 512], "float32"),
+    "land_a": ("sbuf", [128, C], "bfloat16"),
+    "land_b": ("sbuf", [128, C], "bfloat16"),
+    "out_a": ("sbuf", [128, C], "bfloat16"),
+    "out_b0": ("sbuf", [128, H], "bfloat16"),
+    "out_b1": ("sbuf", [128, H], "bfloat16"),
+    "ps_a": ("psum", [128, 512], "float32"),
+    "ps_b0": ("psum", [128, 512], "float32"),
+    "ps_b1": ("psum", [128, 512], "float32"),
 }
-SEMAPHORES = ["loaded", "sent", "from_p", "from_n", "mm_p", "mm_n", "cp_p", "cp_n", "st_p", "st_n"]
-
-
-def _engines(mask, first, count):
-    bits = [b for b in range(mask.bit_length()) if (mask >> b) & 1][first:first + count]
-    return sum(1 << b for b in bits)
+SEMAPHORES = ["staged", "loaded", "sent", "arr_a", "arr_b0", "arr_b1", "mm_a", "mm_b0", "mm_b1",
+              "cp_a", "cp_b0", "cp_b1", "st_a", "st_b0", "st_b1"]
 
 
 def _links(topo, a, b):
     return int(topo.rack(topo.host(a)) != topo.rack(topo.host(b))) + int(topo.chip(a) != topo.chip(b))
 
 
+def _turns(topo, cores, r):
+    n = len(cores)
+    return sorted(((r - 1) % n, (r + 1) % n), key=lambda s: -_links(topo, cores[r], cores[s]))
+
+
+def _mask(topo, src, dst, first):
+    allowed = topo.mask(src, dst)
+    bits = [b for b in range(allowed.bit_length()) if (allowed >> b) & 1]
+    if first:
+        bits = bits[0::2]
+    return sum(1 << b for b in bits), len(bits)
+
+
 def rank_program(g, core, T, topo):
     rank = T.rank_of(core)
     if rank is None:
         return
-    n = len(T.cores)
-    prev, nxt = T.cores[(rank - 1) % n], T.cores[(rank + 1) % n]
-    k = ENGINES_A_TRANSFER
+    cores = T.cores
+    n = len(cores)
     S = T.sem
+    far, near = _turns(topo, cores, rank)
+    assert _turns(topo, cores, far)[0] == rank and _turns(topo, cores, near)[1] == rank
 
-    g.sync.dma_start(T.xs[:], T.x[:]).then_inc(S.loaded, 16)
+    g.sync.dma_start(T.xd[:], T.x[:]).then_inc(S.staged, 16)
+    g.scalar.dma_start(T.xs[:], T.x[:]).then_inc(S.loaded, 16)
 
+    rid_a, pid_a = topo.addr(cores[far], core)
+    rid_b, pid_b = topo.addr(cores[near], core)
+    mask_a, k_a = _mask(topo, core, cores[far], True)
+    mask_b, k_b = _mask(topo, core, cores[near], False)
+    g.wait_ge(S.staged, 16)
+    g.remote_dma(T.land_a[:], T.xd[:], S.arr_a, S.sent, pid_a, rid_a, mask_a)
     g.wait_ge(S.loaded, 16)
-    transfers = []
-    for i, (dst, land, sem) in enumerate(((nxt, T.land_p, S.from_p), (prev, T.land_n, S.from_n))):
-        rid, pid = topo.addr(dst, core)
-        transfers.append(RemoteDMATransfer(dst_ids=[DstId(rid=rid, pnc=pid)],
-                                           dma_engine_mask=_engines(topo.mask(core, dst), i * k, k),
-                                           remote_sem=sem, src=T.xs[:], dst=land[:]))
-    g.remote_dma_fused(transfers, local_sem=S.sent)
+    g.remote_dma(T.land_b[:, 0:H], T.xs[:, 0:H], S.arr_b0, S.sent, pid_b, rid_b, mask_b)
+    g.remote_dma(T.land_b[:, H:C], T.xs[:, H:C], S.arr_b1, S.sent, pid_b, rid_b, mask_b)
 
-    blocks = [
-        (prev, T.land_p, S.from_p, T.ps_p, S.mm_p, T.out_p, S.cp_p, S.st_p, 0),
-        (nxt, T.land_n, S.from_n, T.ps_n, S.mm_n, T.out_n, S.cp_n, S.st_n, 2),
-    ]
-    blocks.sort(key=lambda b: _links(topo, b[0], core))
+    in_a = _mask(topo, cores[far], core, True)[1]
+    in_b = _mask(topo, cores[near], core, False)[1]
+    col_a = (0 if far == (rank - 1) % n else 2) * C
+    col_b = (0 if near == (rank - 1) % n else 2) * C
+
     g.tensor.wait_ge(S.loaded, 16)
-    for q, (src, land, arrived, ps, mm, out, cp, st, blk) in zip((g.sync, g.scalar), blocks):
-        g.tensor.wait_ge(arrived, k)
-        g.tensor.matmul(ps[:, 0:C], T.xs[:], land[:], True, True).then_inc(mm, 1)
-        g.vector.wait_ge(mm, 1)
-        g.vector.tensor_copy(out[:], ps[:, 0:C]).then_inc(cp, 1)
-        q.wait_ge(cp, 1)
-        q.dma_start(T.y[:, blk * C:(blk + 1) * C], out[:]).then_inc(st, 16)
-        q.wait_ge(st, 16)
+    g.tensor.wait_ge(S.arr_a, in_a)
+    g.tensor.matmul(T.ps_a[:, 0:C], T.xs[:], T.land_a[:], True, True).then_inc(S.mm_a, 1)
+    g.tensor.wait_ge(S.arr_b0, in_b)
+    g.tensor.matmul(T.ps_b0[:, 0:H], T.xs[:], T.land_b[:, 0:H], True, True).then_inc(S.mm_b0, 1)
+    g.tensor.wait_ge(S.arr_b1, in_b)
+    g.tensor.matmul(T.ps_b1[:, 0:H], T.xs[:], T.land_b[:, H:C], True, True).then_inc(S.mm_b1, 1)
 
-    g.wait_ge(S.sent, 2 * k)
+    g.vector.wait_ge(S.mm_a, 1)
+    g.vector.tensor_copy(T.out_a[:], T.ps_a[:, 0:C]).then_inc(S.cp_a, 1)
+    g.vector.wait_ge(S.mm_b0, 1)
+    g.vector.tensor_copy(T.out_b0[:], T.ps_b0[:, 0:H]).then_inc(S.cp_b0, 1)
+    g.vector.wait_ge(S.mm_b1, 1)
+    g.vector.tensor_copy(T.out_b1[:], T.ps_b1[:, 0:H]).then_inc(S.cp_b1, 1)
+
+    g.scalar.wait_ge(S.cp_a, 1)
+    g.scalar.dma_start(T.y[:, col_a:col_a + C], T.out_a[:]).then_inc(S.st_a, 16)
+    g.scalar.wait_ge(S.cp_b0, 1)
+    g.scalar.dma_start(T.y[:, col_b:col_b + H], T.out_b0[:]).then_inc(S.st_b0, 16)
+    g.sync.wait_ge(S.cp_b1, 1)
+    g.sync.dma_start(T.y[:, col_b + H:col_b + C], T.out_b1[:]).then_inc(S.st_b1, 16)
+
+    g.scalar.wait_ge(S.st_a, 16)
+    g.scalar.wait_ge(S.st_b0, 16)
+    g.sync.wait_ge(S.st_b1, 16)
+
+    g.wait_ge(S.sent, k_a + 2 * k_b)

C = 128
H = C // 2

SCRATCH = {
    "xd": ("dram", [128, C], "bfloat16"),
    "xs": ("sbuf", [128, C], "bfloat16"),
    "land_a": ("sbuf", [128, C], "bfloat16"),
    "land_b": ("sbuf", [128, C], "bfloat16"),
    "out_a": ("sbuf", [128, C], "bfloat16"),
    "out_b0": ("sbuf", [128, H], "bfloat16"),
    "out_b1": ("sbuf", [128, H], "bfloat16"),
    "ps_a": ("psum", [128, 512], "float32"),
    "ps_b0": ("psum", [128, 512], "float32"),
    "ps_b1": ("psum", [128, 512], "float32"),
}
SEMAPHORES = ["staged", "loaded", "sent", "arr_a", "arr_b0", "arr_b1", "mm_a", "mm_b0", "mm_b1",
              "cp_a", "cp_b0", "cp_b1", "st_a", "st_b0", "st_b1"]


def _links(topo, a, b):
    return int(topo.rack(topo.host(a)) != topo.rack(topo.host(b))) + int(topo.chip(a) != topo.chip(b))


def _turns(topo, cores, r):
    n = len(cores)
    return sorted(((r - 1) % n, (r + 1) % n), key=lambda s: -_links(topo, cores[r], cores[s]))


def _mask(topo, src, dst, first):
    allowed = topo.mask(src, dst)
    bits = [b for b in range(allowed.bit_length()) if (allowed >> b) & 1]
    if first:
        bits = bits[0::2]
    return sum(1 << b for b in bits), len(bits)


def rank_program(g, core, T, topo):
    rank = T.rank_of(core)
    if rank is None:
        return
    cores = T.cores
    n = len(cores)
    S = T.sem
    far, near = _turns(topo, cores, rank)
    assert _turns(topo, cores, far)[0] == rank and _turns(topo, cores, near)[1] == rank

    g.sync.dma_start(T.xd[:], T.x[:]).then_inc(S.staged, 16)
    g.scalar.dma_start(T.xs[:], T.x[:]).then_inc(S.loaded, 16)

    rid_a, pid_a = topo.addr(cores[far], core)
    rid_b, pid_b = topo.addr(cores[near], core)
    mask_a, k_a = _mask(topo, core, cores[far], True)
    mask_b, k_b = _mask(topo, core, cores[near], False)
    g.wait_ge(S.staged, 16)
    g.remote_dma(T.land_a[:], T.xd[:], S.arr_a, S.sent, pid_a, rid_a, mask_a)
    g.wait_ge(S.loaded, 16)
    g.remote_dma(T.land_b[:, 0:H], T.xs[:, 0:H], S.arr_b0, S.sent, pid_b, rid_b, mask_b)
    g.remote_dma(T.land_b[:, H:C], T.xs[:, H:C], S.arr_b1, S.sent, pid_b, rid_b, mask_b)

    in_a = _mask(topo, cores[far], core, True)[1]
    in_b = _mask(topo, cores[near], core, False)[1]
    col_a = (0 if far == (rank - 1) % n else 2) * C
    col_b = (0 if near == (rank - 1) % n else 2) * C

    g.tensor.wait_ge(S.loaded, 16)
    g.tensor.wait_ge(S.arr_a, in_a)
    g.tensor.matmul(T.ps_a[:, 0:C], T.xs[:], T.land_a[:], True, True).then_inc(S.mm_a, 1)
    g.tensor.wait_ge(S.arr_b0, in_b)
    g.tensor.matmul(T.ps_b0[:, 0:H], T.xs[:], T.land_b[:, 0:H], True, True).then_inc(S.mm_b0, 1)
    g.tensor.wait_ge(S.arr_b1, in_b)
    g.tensor.matmul(T.ps_b1[:, 0:H], T.xs[:], T.land_b[:, H:C], True, True).then_inc(S.mm_b1, 1)

    g.vector.wait_ge(S.mm_a, 1)
    g.vector.tensor_copy(T.out_a[:], T.ps_a[:, 0:C]).then_inc(S.cp_a, 1)
    g.vector.wait_ge(S.mm_b0, 1)
    g.vector.tensor_copy(T.out_b0[:], T.ps_b0[:, 0:H]).then_inc(S.cp_b0, 1)
    g.vector.wait_ge(S.mm_b1, 1)
    g.vector.tensor_copy(T.out_b1[:], T.ps_b1[:, 0:H]).then_inc(S.cp_b1, 1)

    g.scalar.wait_ge(S.cp_a, 1)
    g.scalar.dma_start(T.y[:, col_a:col_a + C], T.out_a[:]).then_inc(S.st_a, 16)
    g.scalar.wait_ge(S.cp_b0, 1)
    g.scalar.dma_start(T.y[:, col_b:col_b + H], T.out_b0[:]).then_inc(S.st_b0, 16)
    g.sync.wait_ge(S.cp_b1, 1)
    g.sync.dma_start(T.y[:, col_b + H:col_b + C], T.out_b1[:]).then_inc(S.st_b1, 16)

    g.scalar.wait_ge(S.st_a, 16)
    g.scalar.wait_ge(S.st_b0, 16)
    g.sync.wait_ge(S.st_b1, 16)

    g.wait_ge(S.sent, k_a + 2 * k_b)
